import numpy as np
import ml_dtypes

BF16 = ml_dtypes.bfloat16


def bf(x):
    return np.asarray(x, np.float32).astype(BF16)


def f32(x):
    return np.asarray(x, np.float32)


def f64(x):
    return np.asarray(x).astype(np.float64)


def striped(idx):
    return np.tile(idx.reshape(-1, 16).T, (8, 1))


S, K, M, N, B, Q = 512, 128, 128, 256, 2, 128


def setup_inputs():
    return {"base": bf(np.random.standard_normal((B, M, S))), "x": bf(np.random.standard_normal((K, N))), "w": bf(np.random.standard_normal((K, M)) / np.sqrt(K)), "b": f32(0.5 * np.random.standard_normal((M, 1))), "offs": striped(np.random.permutation(S)[:N])}


def reference(base, x, w, b, offs):
    idx = offs[:16].T.reshape(-1)
    z = f64(base).copy()
    for i in range(B):
        z[i][:, idx[i * Q : (i + 1) * Q]] = f64(w).T @ f64(x)[:, i * Q : (i + 1) * Q]
    return z + f64(b)

@@ -1,0 +1,53 @@
+import concourse.mybir as mybir
+from concourse.masks import make_identity
+
+BF16, F32, U16 = mybir.dt.bfloat16, mybir.dt.float32, mybir.dt.uint16
+
+P = 128
+SEQS = 2
+TOKENS = 512
+PIECE = 128
+PIECE_COLS = PIECE // 16
+
+FLOPS = 2 * P * P * SEQS * PIECE
+
+
+def tile_scatter_matmul_kernel(tc, base, x, w, b, offs, out):
+    nc = tc.nc
+    with (
+        tc.tile_pool(name="held", bufs=1) as held,
+        tc.psum_pool(name="windows", bufs=1) as windows,
+    ):
+        offsets = held.tile([P, SEQS * PIECE_COLS], U16, name="offsets")
+        base_tiles = [held.tile([P, TOKENS], BF16, name=f"base{i}") for i in range(SEQS)]
+        x_tile = held.tile([P, SEQS * PIECE], BF16, name="x_tile")
+        w_tile = held.tile([P, P], BF16, name="w_tile")
+        bias = held.tile([P, 1], F32, name="bias")
+        ident = held.tile([P, P], BF16, name="ident")
+
+        nc.sync.dma_start(base_tiles[0][:], base[0])
+        nc.scalar.dma_start(base_tiles[1][:], base[1])
+        nc.sync.dma_start(offsets[:], offs)
+        nc.scalar.dma_start(w_tile[:], w)
+        nc.sync.dma_start(x_tile[:], x)
+        nc.scalar.dma_start(bias[:], b)
+        make_identity(nc, ident[:])
+
+        window = [windows.tile([P, TOKENS], F32, name=f"window{i}") for i in range(SEQS)]
+        for i in range(SEQS):
+            nc.tensor.matmul(window[i][:], ident[:], base_tiles[i][:], start=True, stop=True)
+
+        for i in range(SEQS):
+            nc.tensor.matmul(
+                window[i][:].indirect(offsets[:, i * PIECE_COLS : (i + 1) * PIECE_COLS]),
+                w_tile[:],
+                x_tile[:, i * PIECE : (i + 1) * PIECE],
+                start=True,
+                stop=True,
+            )
+
+        result = [held.tile([P, TOKENS], F32, name=f"result{i}") for i in range(SEQS)]
+        nc.vector.tensor_scalar(result[0][:], window[0][:], bias[:, 0:1], None, mybir.AluOpType.add)
+        nc.scalar.activation(result[1][:], window[1][:], mybir.ActivationFunctionType.Identity, bias=bias[:, 0:1])
+        nc.sync.dma_start(out[0], result[0][:])
+        nc.scalar.dma_start(out[1], result[1][:])

@@ -33,6 +33,10 @@ def tile_scatter_matmul_kernel(tc, base, x, w, b, offs, out):
         nc.scalar.dma_start(bias[:], b)
         make_identity(nc, ident[:])
 
+        warm = held.tile([P, 1], F32, name="warm")
+        nc.vector.memset(warm[:], 0.0)
+        nc.scalar.activation(warm[:], warm[:], mybir.ActivationFunctionType.Identity)
+
         window = [windows.tile([P, TOKENS], F32, name=f"window{i}") for i in range(SEQS)]
         for i in range(SEQS):
             nc.tensor.matmul(window[i][:], ident[:], base_tiles[i][:], start=True, stop=True)

@@ -6,6 +6,7 @@ BF16, F32, U16 = mybir.dt.bfloat16, mybir.dt.float32, mybir.dt.uint16
 P = 128
 SEQS = 2
 TOKENS = 512
+WARM_MATMULS = 12
 PIECE = 128
 PIECE_COLS = PIECE // 16
 
@@ -24,6 +25,12 @@ def tile_scatter_matmul_kernel(tc, base, x, w, b, offs, out):
         w_tile = held.tile([P, P], BF16, name="w_tile")
         bias = held.tile([P, 1], F32, name="bias")
         ident = held.tile([P, P], BF16, name="ident")
+
+        zeros = held.tile([P, P], BF16, name="zeros")
+        nc.vector.memset(zeros[:], 0.0)
+        unread = windows.tile([P, P], F32, name="unread")
+        for warm_pass in range(WARM_MATMULS):
+            nc.tensor.matmul(unread[:], zeros[:], zeros[:], start=True, stop=True)
 
         nc.sync.dma_start(base_tiles[0][:], base[0])
         nc.scalar.dma_start(base_tiles[1][:], base[1])

@@ -9,6 +9,7 @@ TOKENS = 512
 WARM_MATMULS = 12
 PIECE = 128
 PIECE_COLS = PIECE // 16
+BLOCK = 32
 
 FLOPS = 2 * P * P * SEQS * PIECE
 
@@ -23,7 +24,8 @@ def tile_scatter_matmul_kernel(tc, base, x, w, b, offs, out):
         base_tiles = [held.tile([P, TOKENS], BF16, name=f"base{i}") for i in range(SEQS)]
         x_tile = held.tile([P, SEQS * PIECE], BF16, name="x_tile")
         w_tile = held.tile([P, P], BF16, name="w_tile")
-        bias = held.tile([P, 1], F32, name="bias")
+        bias_rows = held.tile([P, BLOCK], F32, name="bias_rows", align_bytes=64)
+        bias_cols = held.tile([P, BLOCK], F32, name="bias_cols", align_bytes=64)
         ident = held.tile([P, P], BF16, name="ident")
 
         zeros = held.tile([P, P], BF16, name="zeros")
@@ -32,17 +34,21 @@ def tile_scatter_matmul_kernel(tc, base, x, w, b, offs, out):
         for warm_pass in range(WARM_MATMULS):
             nc.tensor.matmul(unread[:], zeros[:], zeros[:], start=True, stop=True)
 
+        nc.vector.memset(bias_rows[:], 0.0)
         nc.sync.dma_start(base_tiles[0][:], base[0])
         nc.scalar.dma_start(base_tiles[1][:], base[1])
         nc.sync.dma_start(offsets[:], offs)
         nc.scalar.dma_start(w_tile[:], w)
         nc.sync.dma_start(x_tile[:], x)
-        nc.scalar.dma_start(bias[:], b)
+        nc.scalar.dma_start(bias_rows[0:P:BLOCK, :], b.rearrange("(q c) o -> q (c o)", c=BLOCK))
         make_identity(nc, ident[:])
 
         warm = held.tile([P, 1], F32, name="warm")
         nc.vector.memset(warm[:], 0.0)
         nc.scalar.activation(warm[:], warm[:], mybir.ActivationFunctionType.Identity)
+
+        nc.vector.transpose(bias_cols[:], bias_rows[:])
+        bias = bias_cols[:, 0:1]
 
         window = [windows.tile([P, TOKENS], F32, name=f"window{i}") for i in range(SEQS)]
         for i in range(SEQS):
@@ -58,7 +64,7 @@ def tile_scatter_matmul_kernel(tc, base, x, w, b, offs, out):
             )
 
         result = [held.tile([P, TOKENS], F32, name=f"result{i}") for i in range(SEQS)]
-        nc.vector.tensor_scalar(result[0][:], window[0][:], bias[:, 0:1], None, mybir.AluOpType.add)
-        nc.scalar.activation(result[1][:], window[1][:], mybir.ActivationFunctionType.Identity, bias=bias[:, 0:1])
+        nc.vector.tensor_scalar(result[0][:], window[0][:], bias, None, mybir.AluOpType.add)
+        nc.scalar.activation(result[1][:], window[1][:], mybir.ActivationFunctionType.Identity, bias=bias)
         nc.sync.dma_start(out[0], result[0][:])
         nc.scalar.dma_start(out[1], result[1][:])

@@ -36,10 +36,10 @@ def tile_scatter_matmul_kernel(tc, base, x, w, b, offs, out):
 
         nc.vector.memset(bias_rows[:], 0.0)
         nc.sync.dma_start(base_tiles[0][:], base[0])
-        nc.scalar.dma_start(base_tiles[1][:], base[1])
-        nc.sync.dma_start(offsets[:], offs)
-        nc.scalar.dma_start(w_tile[:], w)
+        nc.sync.dma_start(base_tiles[1][:], base[1])
         nc.sync.dma_start(x_tile[:], x)
+        nc.sync.dma_start(w_tile[:], w)
+        nc.sync.dma_start(offsets[:], offs)
         nc.scalar.dma_start(bias_rows[0:P:BLOCK, :], b.rearrange("(q c) o -> q (c o)", c=BLOCK))
         make_identity(nc, ident[:])
 

@@ -40,7 +40,7 @@ def tile_scatter_matmul_kernel(tc, base, x, w, b, offs, out):
         nc.sync.dma_start(x_tile[:], x)
         nc.sync.dma_start(w_tile[:], w)
         nc.sync.dma_start(offsets[:], offs)
-        nc.scalar.dma_start(bias_rows[0:P:BLOCK, :], b.rearrange("(q c) o -> q (c o)", c=BLOCK))
+        nc.sync.dma_start(bias_rows[0:P:BLOCK, :], b.rearrange("(q c) o -> q (c o)", c=BLOCK))
         make_identity(nc, ident[:])
 
         warm = held.tile([P, 1], F32, name="warm")

@@ -30,6 +30,7 @@ def tile_scatter_matmul_kernel(tc, base, x, w, b, offs, out):
 
         zeros = held.tile([P, P], BF16, name="zeros")
         nc.vector.memset(zeros[:], 0.0)
+        nc.vector.memset(ident[:], 0.0)
         unread = windows.tile([P, P], F32, name="unread")
         for warm_pass in range(WARM_MATMULS):
             nc.tensor.matmul(unread[:], zeros[:], zeros[:], start=True, stop=True)
@@ -41,7 +42,7 @@ def tile_scatter_matmul_kernel(tc, base, x, w, b, offs, out):
         nc.sync.dma_start(w_tile[:], w)
         nc.sync.dma_start(offsets[:], offs)
         nc.sync.dma_start(bias_rows[0:P:BLOCK, :], b.rearrange("(q c) o -> q (c o)", c=BLOCK))
-        make_identity(nc, ident[:])
+        make_identity(nc, ident[:], nomemset=True)
 
         warm = held.tile([P, 1], F32, name="warm")
         nc.vector.memset(warm[:], 0.0)

import concourse.mybir as mybir
from concourse.masks import make_identity

BF16, F32, U16 = mybir.dt.bfloat16, mybir.dt.float32, mybir.dt.uint16

P = 128
SEQS = 2
TOKENS = 512
WARM_MATMULS = 12
PIECE = 128
PIECE_COLS = PIECE // 16
BLOCK = 32

FLOPS = 2 * P * P * SEQS * PIECE


def tile_scatter_matmul_kernel(tc, base, x, w, b, offs, out):
    nc = tc.nc
    with (
        tc.tile_pool(name="held", bufs=1) as held,
        tc.psum_pool(name="windows", bufs=1) as windows,
    ):
        offsets = held.tile([P, SEQS * PIECE_COLS], U16, name="offsets")
        base_tiles = [held.tile([P, TOKENS], BF16, name=f"base{i}") for i in range(SEQS)]
        x_tile = held.tile([P, SEQS * PIECE], BF16, name="x_tile")
        w_tile = held.tile([P, P], BF16, name="w_tile")
        bias_rows = held.tile([P, BLOCK], F32, name="bias_rows", align_bytes=64)
        bias_cols = held.tile([P, BLOCK], F32, name="bias_cols", align_bytes=64)
        ident = held.tile([P, P], BF16, name="ident")

        zeros = held.tile([P, P], BF16, name="zeros")
        nc.vector.memset(zeros[:], 0.0)
        nc.vector.memset(ident[:], 0.0)
        unread = windows.tile([P, P], F32, name="unread")
        for warm_pass in range(WARM_MATMULS):
            nc.tensor.matmul(unread[:], zeros[:], zeros[:], start=True, stop=True)

        nc.vector.memset(bias_rows[:], 0.0)
        nc.sync.dma_start(base_tiles[0][:], base[0])
        nc.sync.dma_start(base_tiles[1][:], base[1])
        nc.sync.dma_start(x_tile[:], x)
        nc.sync.dma_start(w_tile[:], w)
        nc.sync.dma_start(offsets[:], offs)
        nc.sync.dma_start(bias_rows[0:P:BLOCK, :], b.rearrange("(q c) o -> q (c o)", c=BLOCK))
        make_identity(nc, ident[:], nomemset=True)

        warm = held.tile([P, 1], F32, name="warm")
        nc.vector.memset(warm[:], 0.0)
        nc.scalar.activation(warm[:], warm[:], mybir.ActivationFunctionType.Identity)

        nc.vector.transpose(bias_cols[:], bias_rows[:])
        bias = bias_cols[:, 0:1]

        window = [windows.tile([P, TOKENS], F32, name=f"window{i}") for i in range(SEQS)]
        for i in range(SEQS):
            nc.tensor.matmul(window[i][:], ident[:], base_tiles[i][:], start=True, stop=True)

        for i in range(SEQS):
            nc.tensor.matmul(
                window[i][:].indirect(offsets[:, i * PIECE_COLS : (i + 1) * PIECE_COLS]),
                w_tile[:],
                x_tile[:, i * PIECE : (i + 1) * PIECE],
                start=True,
                stop=True,
            )

        result = [held.tile([P, TOKENS], F32, name=f"result{i}") for i in range(SEQS)]
        nc.vector.tensor_scalar(result[0][:], window[0][:], bias, None, mybir.AluOpType.add)
        nc.scalar.activation(result[1][:], window[1][:], mybir.ActivationFunctionType.Identity, bias=bias)
        nc.sync.dma_start(out[0], result[0][:])
        nc.scalar.dma_start(out[1], result[1][:])
